import numpy as np
import ml_dtypes


def mxq(x, axis, fmt="e4m3"):
    dtype, down = {"e4m3": (ml_dtypes.float8_e4m3fn, 7), "e5m2": (ml_dtypes.float8_e5m2, 14)}[fmt]
    v = np.moveaxis(np.asarray(x, np.float32).astype(ml_dtypes.bfloat16).astype(np.float64), axis, -1)
    blocks = v.reshape(v.shape[:-1] + (-1, 32))
    amax = np.abs(blocks).max(-1, keepdims=True)
    byte = np.maximum(np.where(amax > 0, np.frexp(amax)[1] - 1 + 127, 0) - down, 1)
    scale = np.exp2(byte - 127.0)
    codes = (blocks / scale).astype(np.float32).astype(dtype).astype(np.float64)
    return np.moveaxis((codes * scale).reshape(v.shape), -1, axis)


WIDE = False


def mx_kscale(k):
    if not WIDE:
        return np.ones(k)
    levels = np.array([10, -10, 5, -5, 0])
    if k % 512:
        return np.exp2(np.random.permutation(np.resize(levels, k // 32))).repeat(32)
    a = np.empty((k // 512, 16))
    for p in range(k // 512):
        a[p, :8] = np.random.permutation(np.resize(levels, 8))
        for g in range(8):
            far = levels[np.abs(levels - a[p, g]) >= 10]
            a[p, g + 8] = far[np.random.randint(len(far))]
    return np.exp2(a.ravel()).repeat(32)


BF16 = ml_dtypes.bfloat16


def bf(x):
    return np.asarray(x, np.float32).astype(BF16)


def f64(x):
    return np.asarray(x).astype(np.float64)


E2M1 = np.array([0.0, 0.5, 1.0, 1.5, 2.0, 3.0, 4.0, 6.0, -0.0, -0.5, -1.0, -1.5, -2.0, -3.0, -4.0, -6.0])


def pack_weight(w, fmt):
    k, n = w.shape
    w = f64(bf(w)).reshape(k // 32, 32, n)
    amax = np.abs(w).max(1)
    if fmt == "e4m3":
        byte = np.frexp(amax)[1] - 1 + 127 - 7
    else:
        mant, ex = np.frexp(amax / 6.0)
        byte = np.where(mant > 0.5, ex, ex - 1) + 127
    byte = np.clip(np.where(amax > 0, byte, 1), 1, 254)
    scaled = (w * np.exp2(127.0 - byte)[:, None, :]).reshape(k, n).astype(np.float32)
    by_word = np.ascontiguousarray(scaled.reshape(k // 512, 128, 4, n).transpose(0, 1, 3, 2))
    if fmt == "e4m3":
        words = by_word.astype(ml_dtypes.float8_e4m3fn).view(np.uint8)
    else:
        c = by_word.astype(ml_dtypes.float4_e2m1fn).view(np.uint8) & 0xF
        words = c[..., 0::2] | (c[..., 1::2] << 4)
    return np.ascontiguousarray(words), np.ascontiguousarray(byte.astype(np.uint8).reshape(k // 512, 16, n))


def unpack_weight(words, scales, fmt):
    g, p, n, _ = words.shape
    if fmt == "e4m3":
        vals = np.ascontiguousarray(words).view(ml_dtypes.float8_e4m3fn).astype(np.float64)
    else:
        nib = np.empty((g, p, n, 4), np.uint8)
        nib[..., 0::2] = words & 0xF
        nib[..., 1::2] = words >> 4
        vals = E2M1[nib]
    vals = vals * np.repeat(np.exp2(scales.astype(np.float64) - 127.0), 8, axis=1)[..., None]
    return vals.transpose(0, 1, 3, 2).reshape(g * 512, n)
def pack4(w):
    words, scales = pack_weight(w, "e2m1")
    return words.reshape(words.shape[0], 128, -1), scales


def unpack4(words, scales):
    return unpack_weight(words.reshape(words.shape[0], 128, -1, 2), scales, "e2m1")


def planes(Y):
    n, m = Y.shape
    b = f64(bf(Y)).reshape(n // 32, 32, m)
    amax = np.abs(b).max(1)
    byte = np.clip(np.where(amax > 0, np.frexp(amax)[1] - 1 + 127 - 7, 1), 1, 254)
    codes = (b * np.exp2(127.0 - byte)[:, None, :]).reshape(n, m).astype(np.float32).astype(ml_dtypes.float8_e4m3fn).view(np.uint8)
    words = codes.reshape(n // 512, 128, 4, m).transpose(0, 1, 3, 2)
    return np.ascontiguousarray(words), np.ascontiguousarray(byte.astype(np.uint8).reshape(n // 512, 16, m))


T, D, F, E = 1024, 1536, 2048, 512
GELU_C = np.sqrt(2.0 / np.pi)


def gelu(u):
    return 0.5 * u * (1.0 + np.tanh(GELU_C * (u + 0.044715 * u * u * u)))


def setup_inputs():
    rn = np.random.standard_normal
    s = mx_kscale(D)
    t = mx_kscale(F)
    x = bf(rn((T, D)) * s)
    w1 = f64(bf(rn((D, F)) / np.sqrt(D) / s[:, None]))
    a = bf((1.0 + 0.2 * rn(F)) * t)
    w2 = f64(bf(1.5 * rn((F, E)) / np.sqrt(F) / t[:, None]))
    w1_words, w1_scales = pack4(w1)
    w2_words, w2_scales = pack4(w2)
    b = bf(0.3 * rn(E))
    c = bf(np.exp(0.8 * rn(E)))
    r = bf(np.exp(0.3 * rn(T)))
    return {"x": x, "w1_words": w1_words, "w1_scales": w1_scales, "a": a,
            "w2_words": w2_words, "w2_scales": w2_scales, "b": b, "c": c, "r": r}


def reference(x, w1_words, w1_scales, a, w2_words, w2_scales, b, c, r):
    u = mxq(f64(x), 1, "e4m3") @ unpack4(w1_words, w1_scales)
    h = gelu(u) * f64(a)
    z = mxq(h, 1, "e4m3") @ unpack4(w2_words, w2_scales)
    y = (z + f64(b)) * f64(c) * f64(r)[:, None]
    Y = y.T
    words, scales = planes(Y)
    return y, words, scales

@@ -1,0 +1,404 @@
+from contextlib import ExitStack
+
+import concourse.mybir as mybir
+from concourse.masks import make_identity
+
+T, D, F, E = 1024, 1536, 2048, 512
+FLOPS = 2 * T * D * F + 2 * T * F * E
+
+F32 = mybir.dt.float32
+BF16 = mybir.dt.bfloat16
+I32 = mybir.dt.int32
+U32 = mybir.dt.uint32
+U8 = mybir.dt.uint8
+FP8X4 = mybir.dt.float8_e4m3fn_x4
+FP4X4 = mybir.dt.float4_e2m1fn_x4
+GELU = mybir.ActivationFunctionType.Gelu_apprx_tanh
+COPY = mybir.ActivationFunctionType.Copy
+ADD = mybir.AluOpType.add
+MULT = mybir.AluOpType.mult
+
+P = 128
+PACK = 4
+KP = P * PACK
+HALF = 512
+TILES = HALF // P
+G1 = D // KP
+G2 = F // KP
+
+
+def tile_masked_token_embedding_head_h1_kernel(
+    tc, x, w1_words, w1_scales, a, w2_words, w2_scales, b, c, r, out_0, out_1, out_2
+):
+    nc = tc.nc
+    with ExitStack() as ctx:
+        keep = ctx.enter_context(tc.tile_pool(name="keep", bufs=1))
+        work = ctx.enter_context(tc.tile_pool(name="work", bufs=2))
+        psum = ctx.enter_context(tc.psum_pool(name="psum", bufs=4))
+        ctx.enter_context(tc.manual_schedule())
+
+        def kept(name, shape, dtype):
+            return keep.tile(shape, dtype, name=name, align_bytes=64)
+
+        ident = kept("ident", [P, P], F32)
+        make_identity(nc, ident[:])
+
+        x_raw = {}
+        xg = {}
+        xq = {}
+        xs = {}
+        w1_raw = {}
+        w1p = {}
+        s1p = {}
+        gel = {}
+        hb = {}
+        hc = {}
+        hq = {}
+        hs = {}
+        zb = {}
+        tb = {}
+        ys = {}
+        yb = {}
+        ytb = {}
+
+        s1_first = kept("s1_first", [P, G1, KP], U8)
+        s1_rest = kept("s1_rest", [P, G1, F - KP], U8)
+        s2 = kept("s2", [P, G2, E], U8)
+        w2 = kept("w2", [P, G2, 2 * E], U8)
+        a_sb = kept("a_sb", [P, G2, PACK], BF16)
+        a32 = None
+        b_sb = kept("b_sb", [P, E], BF16)
+        c_sb = kept("c_sb", [P, E], BF16)
+        r_sb = kept("r_sb", [P, T // P, 2], BF16)
+        yq = kept("yq", [P, T], U32)
+        yscale = kept("yscale", [P, T], U8)
+        yt = {0: kept("yt0", [P, HALF * PACK], BF16)}
+        for i in range(2):
+            yt[1, i] = kept("yt1_%d" % i, [P, 2 * P * PACK], BF16)
+
+        for plane in (s1_first, s1_rest, s2):
+            nc.vector.memset(plane[:].rearrange("p g n -> p (g n)").bitcast(I32), 0)
+
+        def load_x(h, g):
+            x_raw[h, g] = kept("x_%d_%d" % (h, g), [P, TILES, KP], BF16)
+            rows = x[h * HALF : (h + 1) * HALF, g * KP : (g + 1) * KP]
+            nc.sync.dma_start(out=x_raw[h, g][:], in_=rows.rearrange("(i p) k -> p i k", p=P))
+
+        def load_w1(G, g0, g1):
+            raw = kept("w1_%d_%d" % (G, g0), [P, g1 - g0, 2 * KP], U8)
+            src = w1_words[g0:g1, :, 2 * KP * G : 2 * KP * (G + 1)]
+            nc.sync.dma_start(out=raw[:].bitcast(I32), in_=src.rearrange("g p n -> p g n").bitcast(I32))
+            for g in range(g0, g1):
+                w1_raw[G, g] = raw[:, g - g0, :]
+
+        def load_scales(plane, rows):
+            for q in range(4):
+                nc.sync.dma_start(
+                    out=plane[32 * q : 32 * q + 4, :, :].bitcast(I32),
+                    in_=rows[:, 4 * q : 4 * q + 4, :].rearrange("g r n -> r g n").bitcast(I32),
+                )
+
+        def sort_scales(G, g):
+            if G == 0:
+                src = s1_first[:, g, :]
+            else:
+                src = s1_rest[:, g, (G - 1) * KP : G * KP]
+            s1p[G, g] = kept("s1p_%d_%d" % (G, g), [P, PACK, P], U8)
+            nc.vector.tensor_copy(out=s1p[G, g][:], in_=src.rearrange("p (m t) -> p t m", t=PACK))
+
+        def sort_words(G, g):
+            w1p[G, g] = kept("w1p_%d_%d" % (G, g), [P, PACK, 2 * P], U8)
+            nc.vector.tensor_copy(
+                out=w1p[G, g][:].rearrange("p t (m e) -> p t m e", e=2),
+                in_=w1_raw[G, g].rearrange("p (m t e) -> p t m e", t=PACK, e=2),
+            )
+
+        def sort_group(G):
+            for g in range(G1):
+                sort_words(G, g)
+                sort_scales(G, g)
+
+        def turn_x(h, g, second=nc.scalar.copy):
+            xg[h, g] = work.tile([P, HALF * PACK], BF16, name="xg", bufs=3, align_bytes=64)
+            dst = xg[h, g][:].bitcast(F32)
+            for pair in range(TILES // 2):
+                bank = psum.tile([P, 2, 2, P], F32, name="aux")
+                for ii in range(2):
+                    words = x_raw[h, g][:, 2 * pair + ii, :].bitcast(F32)
+                    for u in range(2):
+                        nc.tensor.transpose(bank[:, ii, u, :], words[:, u : 2 * P : 2], ident[:])
+                move = nc.scalar.copy if pair == 0 else second
+                move(
+                    out=dst[:, pair * KP : (pair + 1) * KP].rearrange("p (i n u) -> p i n u", i=2, u=2),
+                    in_=bank[:].rearrange("p i u n -> p i n u"),
+                )
+
+        def quant_x(h, g):
+            xq[h, g] = kept("xq_%d_%d" % (h, g), [P, HALF], U32)
+            xs[h, g] = kept("xs_%d_%d" % (h, g), [P, HALF], U8)
+            nc.vector.quantize_mx(out=xq[h, g][:].bitcast(FP8X4), scales=xs[h, g][:], in_=xg[h, g][:])
+
+        def pass1(bank, h, G, g, t, cols):
+            nc.tensor.matmul_mx(
+                out=bank,
+                lhsT=w1p[G, g][:, t, :].bitcast(FP4X4),
+                lhsT_scale=s1p[G, g][:, t, :],
+                rhs=xq[h, g][:, cols].bitcast(FP8X4),
+                rhs_scale=xs[h, g][:, cols],
+                start=(g == 0),
+                stop=(g == G1 - 1),
+            )
+
+        def stage1(h, G):
+            gel[h, G] = work.tile([P, PACK, HALF], F32, name="gel", bufs=4)
+            for t in range(PACK):
+                bank = psum.tile([P, HALF], F32, name="s1")
+                for g in range(G1):
+                    pass1(bank[:], h, G, g, t, slice(0, HALF))
+                nc.scalar.activation(out=gel[h, G][:, t, :], in_=bank[:], func=GELU)
+
+        def scale_h(h, G):
+            hb[h, G] = work.tile([P, HALF * PACK], BF16, name="hb", bufs=3, align_bytes=64)
+            nc.vector.tensor_tensor(
+                out=hb[h, G][:].rearrange("p (n i t) -> p n t i", i=2, t=PACK),
+                in0=gel[h, G][:].rearrange("p t (n i) -> p n t i", i=2),
+                in1=a_sb[:, G, :].unsqueeze(1).unsqueeze(3).broadcast_to([P, HALF // 2, PACK, 2]),
+                op=MULT,
+            )
+
+        def scale_rows(h, G):
+            hc[h, G] = work.tile([P, PACK, HALF], BF16, name="hc", bufs=2)
+            for t in range(PACK):
+                nc.scalar.activation(out=hc[h, G][:, t, :], in_=gel[h, G][:, t, :], func=COPY, scale=a32[:, G, t : t + 1])
+
+        def weave_h(h, G):
+            hb[h, G] = work.tile([P, HALF * PACK], BF16, name="hb", bufs=3, align_bytes=64)
+            nc.vector.tensor_copy(
+                out=hb[h, G][:].rearrange("p (n i t) -> p n t i", i=4, t=PACK),
+                in_=hc[h, G][:].rearrange("p t (n i) -> p n t i", i=4),
+            )
+
+        def quant_h(h, G):
+            hq[h, G] = kept("hq_%d_%d" % (h, G), [P, HALF], U32)
+            hs[h, G] = kept("hs_%d_%d" % (h, G), [P, HALF], U8)
+            nc.vector.quantize_mx(out=hq[h, G][:].bitcast(FP8X4), scales=hs[h, G][:], in_=hb[h, G][:])
+
+        last = G2 - 1
+
+        def stage1_tile(i):
+            bank = psum.tile([P, PACK, P], F32, name="s1")
+            for t in range(PACK):
+                for g in range(G1):
+                    pass1(bank[:, t, :], 1, last, g, t, slice(i * P, (i + 1) * P))
+            gel[1, last, i] = work.tile([P, P, PACK], F32, name="gel_tile", bufs=4)
+            nc.scalar.activation(out=gel[1, last, i][:], in_=bank[:].rearrange("p t n -> p n t"), func=GELU)
+
+        def scale_tile(i):
+            hb[1, last, i] = work.tile([P, P * PACK], BF16, name="hb_tile", bufs=4, align_bytes=64)
+            nc.vector.tensor_tensor(
+                out=hb[1, last, i][:].rearrange("p (n t) -> p n t", t=PACK),
+                in0=gel[1, last, i][:],
+                in1=a_sb[:, last, :].unsqueeze(1).broadcast_to([P, P, PACK]),
+                op=MULT,
+            )
+
+        def quant_tile(i):
+            hq[1, last, i] = kept("hq_tile_%d" % i, [P, P], U32)
+            hs[1, last, i] = kept("hs_tile_%d" % i, [P, P], U8)
+            nc.vector.quantize_mx(
+                out=hq[1, last, i][:].bitcast(FP8X4), scales=hs[1, last, i][:], in_=hb[1, last, i][:]
+            )
+
+        def stage2(h, i, groups):
+            for G in groups:
+                if G == 0:
+                    zb[h, i] = psum.tile([P, E], F32, name="aux")
+                if (h, G, i) in hq:
+                    codes, scales = hq[h, G, i][:], hs[h, G, i][:]
+                else:
+                    codes, scales = hq[h, G][:, i * P : (i + 1) * P], hs[h, G][:, i * P : (i + 1) * P]
+                nc.tensor.matmul_mx(
+                    out=zb[h, i][:],
+                    lhsT=codes.bitcast(FP8X4),
+                    lhsT_scale=scales,
+                    rhs=w2[:, G, :].bitcast(FP4X4),
+                    rhs_scale=s2[:, G, :],
+                    start=(G == 0),
+                    stop=(G == last),
+                )
+
+        def add_bias(h, i):
+            tb[h, i] = work.tile([P, E], F32, name="tb", bufs=3)
+            nc.vector.tensor_tensor(out=tb[h, i][:], in0=zb[h, i][:], in1=b_sb[:], op=ADD)
+
+        def finish_y(h, i):
+            j = h * TILES + i
+            ys[h, i] = kept("y_%d" % j, [P, E], F32)
+            nc.vector.scalar_tensor_tensor(
+                out=ys[h, i][:], in0=tb[h, i][:], scalar=r_sb[:, j, 0:1], in1=c_sb[:], op0=MULT, op1=MULT
+            )
+            nc.sync.dma_start(out=out_0[j * P : (j + 1) * P, :], in_=ys[h, i][:])
+
+        def round_y(h, i, move=nc.scalar.copy):
+            yb[h, i] = work.tile([P, E], BF16, name="yb", bufs=4)
+            move(
+                out=yb[h, i][:].rearrange("n (u m e) -> n u m e", u=2, e=2),
+                in_=ys[h, i][:].rearrange("n (m u e) -> n u m e", u=2, e=2),
+            )
+
+        def turn_y(h, tiles, dst):
+            bank = psum.tile([P, 2, 2, P], F32, name="s1")
+            for ii, i in enumerate(tiles):
+                words = yb[h, i][:].bitcast(F32)
+                for u in range(2):
+                    nc.tensor.transpose(bank[:, ii, u, :], words[:, u * P : (u + 1) * P], ident[:])
+            n = len(tiles)
+            nc.scalar.copy(
+                out=dst.bitcast(F32).rearrange("p (i n u) -> p i n u", i=n, u=2),
+                in_=bank[:, 0:n, :, :].rearrange("p i u n -> p i n u"),
+            )
+
+        def quant_y(src, col0, cols):
+            nc.vector.quantize_mx(
+                out=yq[:, col0 : col0 + cols].bitcast(FP8X4), scales=yscale[:, col0 : col0 + cols], in_=src
+            )
+            words = out_1[0].rearrange("p m t -> p (m t)").bitcast(I32)
+            nc.sync.dma_start(out=words[:, col0 : col0 + cols], in_=yq[:, col0 : col0 + cols].bitcast(I32))
+
+        def store_scales():
+            for q in range(4):
+                eng = nc.sync if q % 2 == 0 else nc.scalar
+                eng.dma_start(
+                    out=out_2[0, 4 * q : 4 * q + 4, :].bitcast(I32),
+                    in_=yscale[32 * q : 32 * q + 4, :].bitcast(I32),
+                )
+
+        load_x(0, 0)
+        load_scales(s1_first, w1_scales[:, :, 0:KP])
+        load_w1(0, 0, G1)
+        load_x(0, 1)
+        load_x(0, 2)
+        load_w1(1, 0, G1)
+        load_scales(s1_rest, w1_scales[:, :, KP:F])
+        nc.sync.dma_start(out=a_sb[:], in_=a.rearrange("(g p t) -> p g t", p=P, t=PACK))
+        load_x(1, 0)
+        load_w1(2, 0, G1)
+        load_x(1, 1)
+        load_w1(3, 0, G1)
+        load_x(1, 2)
+        nc.sync.dma_start(out=w2[:].bitcast(I32), in_=w2_words.rearrange("g p n -> p g n").bitcast(I32))
+        load_scales(s2, w2_scales)
+        nc.sync.dma_start(out=b_sb[:], in_=b.partition_broadcast(P))
+        nc.sync.dma_start(out=c_sb[:], in_=c.partition_broadcast(P))
+        with nc.allow_non_contiguous_dma(reason="one value of r for each token partition"):
+            nc.sync.dma_start(out=r_sb[:, :, 0:1], in_=r.rearrange("(j p o) -> p j o", p=P, o=1))
+
+        for g in range(G1):
+            sort_scales(0, g)
+        turn_x(0, 0)
+        turn_x(0, 1)
+        turn_x(0, 2)
+        sort_words(0, 0)
+        sort_words(0, 1)
+        sort_words(0, 2)
+        quant_x(0, 0)
+        banks = []
+        for t in range(PACK):
+            bank = psum.tile([P, HALF], F32, name="s1")
+            banks.append(bank)
+            pass1(bank[:], 0, 0, 0, t, slice(0, HALF))
+        quant_x(0, 1)
+        sort_words(1, 0)
+        quant_x(0, 2)
+        gel[0, 0] = work.tile([P, PACK, HALF], F32, name="gel", bufs=4)
+        for t in range(PACK):
+            pass1(banks[t][:], 0, 0, 1, t, slice(0, HALF))
+            pass1(banks[t][:], 0, 0, 2, t, slice(0, HALF))
+            nc.scalar.activation(out=gel[0, 0][:, t, :], in_=banks[t][:], func=GELU)
+
+        sort_words(1, 1)
+        sort_words(1, 2)
+        for g in range(G1):
+            sort_scales(1, g)
+        stage1(0, 1)
+        turn_x(1, 0)
+        sort_group(2)
+        scale_h(0, 0)
+        stage1(0, 2)
+        turn_x(1, 1)
+        sort_group(3)
+        quant_h(0, 0)
+        turn_x(1, 2)
+        stage1(0, 3)
+        scale_h(0, 1)
+        quant_x(1, 0)
+        quant_x(1, 1)
+        quant_h(0, 1)
+        quant_x(1, 2)
+        stage1(1, 0)
+        scale_h(0, 2)
+        scale_h(0, 3)
+        quant_h(0, 2)
+        stage1(1, 1)
+        quant_h(0, 3)
+        scale_h(1, 0)
+        stage2(0, 0, range(G2))
+        stage2(0, 1, range(G2))
+        stage2(0, 2, range(G2))
+        stage1(1, 2)
+        scale_h(1, 1)
+        quant_h(1, 0)
+        add_bias(0, 0)
+        quant_h(1, 1)
+        add_bias(0, 1)
+        finish_y(0, 0)
+        add_bias(0, 2)
+        finish_y(0, 1)
+        stage2(0, 3, range(G2))
+        finish_y(0, 2)
+        scale_h(1, 2)
+        add_bias(0, 3)
+        quant_h(1, 2)
+        finish_y(0, 3)
+        round_y(0, 0)
+        stage1_tile(0)
+        round_y(0, 1)
+        stage1_tile(1)
+        round_y(0, 2)
+        stage1_tile(2)
+        stage1_tile(3)
+        round_y(0, 3)
+        stage2(1, 0, range(last))
+        stage2(1, 1, range(last))
+        scale_tile(0)
+        scale_tile(1)
+        quant_tile(0)
+        scale_tile(2)
+        quant_tile(1)
+        stage2(1, 0, [last])
+        stage2(1, 1, [last])
+        turn_y(0, [0, 1], yt[0][:, 0 : 2 * KP])
+        turn_y(0, [2, 3], yt[0][:, 2 * KP : 4 * KP])
+        scale_tile(3)
+        quant_tile(2)
+        add_bias(1, 0)
+        quant_tile(3)
+        stage2(1, 2, range(G2))
+        stage2(1, 3, range(G2))
+        add_bias(1, 1)
+        finish_y(1, 0)
+        round_y(1, 0)
+        finish_y(1, 1)
+        round_y(1, 1)
+        quant_y(yt[0][:], 0, HALF)
+        add_bias(1, 2)
+        add_bias(1, 3)
+        turn_y(1, [0, 1], yt[1, 0][:])
+        finish_y(1, 2)
+        round_y(1, 2)
+        finish_y(1, 3)
+        quant_y(yt[1, 0][:], HALF, 2 * P)
+        round_y(1, 3, nc.vector.tensor_copy)
+        turn_y(1, [2, 3], yt[1, 1][:])
+        quant_y(yt[1, 1][:], HALF + 2 * P, 2 * P)
+        store_scales()

@@ -45,6 +45,7 @@ def tile_masked_token_embedding_head_h1_kernel(
 
         x_raw = {}
         xg = {}
+        x_sorted = {}
         xq = {}
         xs = {}
         w1_raw = {}
@@ -61,8 +62,8 @@ def tile_masked_token_embedding_head_h1_kernel(
         yb = {}
         ytb = {}
 
-        s1_first = kept("s1_first", [P, G1, KP], U8)
-        s1_rest = kept("s1_rest", [P, G1, F - KP], U8)
+        s1_first = kept("s1_first", [P, G1, 2 * KP], U8)
+        s1_rest = kept("s1_rest", [P, G1, F - 2 * KP], U8)
         s2 = kept("s2", [P, G2, E], U8)
         w2 = kept("w2", [P, G2, 2 * E], U8)
         a_sb = kept("a_sb", [P, G2, PACK], BF16)
@@ -73,8 +74,9 @@ def tile_masked_token_embedding_head_h1_kernel(
         yq = kept("yq", [P, T], U32)
         yscale = kept("yscale", [P, T], U8)
         yt = {0: kept("yt0", [P, HALF * PACK], BF16)}
-        for i in range(2):
-            yt[1, i] = kept("yt1_%d" % i, [P, 2 * P * PACK], BF16)
+        yt[1, 0] = kept("yt1_0", [P, 2 * P * PACK], BF16)
+        yt[1, 2] = kept("yt1_2", [P, P * PACK], BF16)
+        yt[1, 3] = kept("yt1_3", [P, P * PACK], BF16)
 
         for plane in (s1_first, s1_rest, s2):
             nc.vector.memset(plane[:].rearrange("p g n -> p (g n)").bitcast(I32), 0)
@@ -99,10 +101,10 @@ def tile_masked_token_embedding_head_h1_kernel(
                 )
 
         def sort_scales(G, g):
-            if G == 0:
-                src = s1_first[:, g, :]
+            if G < 2:
+                src = s1_first[:, g, G * KP : (G + 1) * KP]
             else:
-                src = s1_rest[:, g, (G - 1) * KP : G * KP]
+                src = s1_rest[:, g, (G - 2) * KP : (G - 1) * KP]
             s1p[G, g] = kept("s1p_%d_%d" % (G, g), [P, PACK, P], U8)
             nc.vector.tensor_copy(out=s1p[G, g][:], in_=src.rearrange("p (m t) -> p t m", t=PACK))
 
@@ -118,6 +120,13 @@ def tile_masked_token_embedding_head_h1_kernel(
                 sort_words(G, g)
                 sort_scales(G, g)
 
+        def sort_x(h, g, move=nc.scalar.copy):
+            x_sorted[h, g] = work.tile([P, TILES, 2, P], F32, name="x_sorted", bufs=3)
+            move(
+                out=x_sorted[h, g][:],
+                in_=x_raw[h, g][:].bitcast(F32).rearrange("n i (m u) -> n i u m", u=2),
+            )
+
         def turn_x(h, g, second=nc.scalar.copy):
             xg[h, g] = work.tile([P, HALF * PACK], BF16, name="xg", bufs=3, align_bytes=64)
             dst = xg[h, g][:].bitcast(F32)
@@ -126,7 +135,11 @@ def tile_masked_token_embedding_head_h1_kernel(
                 for ii in range(2):
                     words = x_raw[h, g][:, 2 * pair + ii, :].bitcast(F32)
                     for u in range(2):
-                        nc.tensor.transpose(bank[:, ii, u, :], words[:, u : 2 * P : 2], ident[:])
+                        if (h, g) in x_sorted:
+                            src = x_sorted[h, g][:, 2 * pair + ii, u, :]
+                        else:
+                            src = words[:, u : 2 * P : 2]
+                        nc.tensor.transpose(bank[:, ii, u, :], src, ident[:])
                 move = nc.scalar.copy if pair == 0 else second
                 move(
                     out=dst[:, pair * KP : (pair + 1) * KP].rearrange("p (i n u) -> p i n u", i=2, u=2),
@@ -149,9 +162,10 @@ def tile_masked_token_embedding_head_h1_kernel(
                 stop=(g == G1 - 1),
             )
 
-        def stage1(h, G):
-            gel[h, G] = work.tile([P, PACK, HALF], F32, name="gel", bufs=4)
-            for t in range(PACK):
+        def stage1(h, G, slots=range(PACK)):
+            if slots[0] == 0:
+                gel[h, G] = work.tile([P, PACK, HALF], F32, name="gel", bufs=4)
+            for t in slots:
                 bank = psum.tile([P, HALF], F32, name="s1")
                 for g in range(G1):
                     pass1(bank[:], h, G, g, t, slice(0, HALF))
@@ -192,6 +206,26 @@ def tile_masked_token_embedding_head_h1_kernel(
                     pass1(bank[:, t, :], 1, last, g, t, slice(i * P, (i + 1) * P))
             gel[1, last, i] = work.tile([P, P, PACK], F32, name="gel_tile", bufs=4)
             nc.scalar.activation(out=gel[1, last, i][:], in_=bank[:].rearrange("p t n -> p n t"), func=GELU)
+
+        def stage1_rows(i):
+            bank = psum.tile([P, PACK, P], F32, name="s1")
+            for t in range(PACK):
+                for g in range(G1):
+                    pass1(bank[:, t, :], 1, last, g, t, slice(i * P, (i + 1) * P))
+            rows = work.tile([P, PACK, P], F32, name="gel_tile", bufs=4)
+            nc.scalar.activation(out=rows[:], in_=bank[:], func=GELU)
+            hc[1, last, i] = work.tile([P, PACK, P], BF16, name="hc_tile", bufs=4)
+            for t in range(PACK):
+                nc.scalar.activation(
+                    out=hc[1, last, i][:, t, :], in_=rows[:, t, :], func=COPY, scale=a32[:, last, t : t + 1]
+                )
+
+        def weave_tile(i):
+            hb[1, last, i] = work.tile([P, P * PACK], BF16, name="hb_tile", bufs=4, align_bytes=64)
+            nc.vector.tensor_copy(
+                out=hb[1, last, i][:].rearrange("p (n i t) -> p n t i", i=4, t=PACK),
+                in_=hc[1, last, i][:].rearrange("p t (n i) -> p n t i", i=4),
+            )
 
         def scale_tile(i):
             hb[1, last, i] = work.tile([P, P * PACK], BF16, name="hb_tile", bufs=4, align_bytes=64)
@@ -262,6 +296,8 @@ def tile_masked_token_embedding_head_h1_kernel(
             nc.vector.quantize_mx(
                 out=yq[:, col0 : col0 + cols].bitcast(FP8X4), scales=yscale[:, col0 : col0 + cols], in_=src
             )
+
+        def store_words(col0, cols):
             words = out_1[0].rearrange("p m t -> p (m t)").bitcast(I32)
             nc.sync.dma_start(out=words[:, col0 : col0 + cols], in_=yq[:, col0 : col0 + cols].bitcast(I32))
 
@@ -274,12 +310,12 @@ def tile_masked_token_embedding_head_h1_kernel(
                 )
 
         load_x(0, 0)
-        load_scales(s1_first, w1_scales[:, :, 0:KP])
+        load_scales(s1_first, w1_scales[:, :, 0 : 2 * KP])
         load_w1(0, 0, G1)
         load_x(0, 1)
         load_x(0, 2)
         load_w1(1, 0, G1)
-        load_scales(s1_rest, w1_scales[:, :, KP:F])
+        load_scales(s1_rest, w1_scales[:, :, 2 * KP : F])
         nc.sync.dma_start(out=a_sb[:], in_=a.rearrange("(g p t) -> p g t", p=P, t=PACK))
         load_x(1, 0)
         load_w1(2, 0, G1)
@@ -302,6 +338,8 @@ def tile_masked_token_embedding_head_h1_kernel(
         sort_words(0, 1)
         sort_words(0, 2)
         quant_x(0, 0)
+        for g in range(G1):
+            sort_scales(1, g)
         banks = []
         for t in range(PACK):
             bank = psum.tile([P, HALF], F32, name="s1")
@@ -318,13 +356,14 @@ def tile_masked_token_embedding_head_h1_kernel(
 
         sort_words(1, 1)
         sort_words(1, 2)
-        for g in range(G1):
-            sort_scales(1, g)
+        sort_x(1, 0)
         stage1(0, 1)
         turn_x(1, 0)
         sort_group(2)
         scale_h(0, 0)
-        stage1(0, 2)
+        stage1(0, 2, range(0, 2))
+        sort_x(1, 2)
+        stage1(0, 2, range(2, 4))
         turn_x(1, 1)
         sort_group(3)
         quant_h(0, 0)
@@ -332,30 +371,31 @@ def tile_masked_token_embedding_head_h1_kernel(
         stage1(0, 3)
         scale_h(0, 1)
         quant_x(1, 0)
-        quant_x(1, 1)
         quant_h(0, 1)
+        quant_x(1, 1)
         quant_x(1, 2)
-        stage1(1, 0)
         scale_h(0, 2)
+        stage1(1, 0)
         scale_h(0, 3)
         quant_h(0, 2)
-        stage1(1, 1)
         quant_h(0, 3)
+        stage1(1, 1, range(0, 2))
         scale_h(1, 0)
         stage2(0, 0, range(G2))
         stage2(0, 1, range(G2))
+        stage1(1, 1, range(2, 4))
         stage2(0, 2, range(G2))
         stage1(1, 2)
-        scale_h(1, 1)
-        quant_h(1, 0)
         add_bias(0, 0)
-        quant_h(1, 1)
+        quant_h(1, 0)
         add_bias(0, 1)
         finish_y(0, 0)
-        add_bias(0, 2)
         finish_y(0, 1)
-        stage2(0, 3, range(G2))
+        scale_h(1, 1)
+        add_bias(0, 2)
+        quant_h(1, 1)
         finish_y(0, 2)
+        stage2(0, 3, range(G2))
         scale_h(1, 2)
         add_bias(0, 3)
         quant_h(1, 2)
@@ -390,15 +430,20 @@ def tile_masked_token_embedding_head_h1_kernel(
         round_y(1, 0)
         finish_y(1, 1)
         round_y(1, 1)
-        quant_y(yt[0][:], 0, HALF)
         add_bias(1, 2)
         add_bias(1, 3)
         turn_y(1, [0, 1], yt[1, 0][:])
         finish_y(1, 2)
         round_y(1, 2)
         finish_y(1, 3)
-        quant_y(yt[1, 0][:], HALF, 2 * P)
+        turn_y(1, [2], yt[1, 2][:])
         round_y(1, 3, nc.vector.tensor_copy)
-        turn_y(1, [2, 3], yt[1, 1][:])
-        quant_y(yt[1, 1][:], HALF + 2 * P, 2 * P)
+        turn_y(1, [3], yt[1, 3][:])
+        quant_y(yt[0][:], 0, HALF)
+        store_words(0, HALF)
+        quant_y(yt[1, 0][:], HALF, 2 * P)
+        store_words(HALF, 2 * P)
+        quant_y(yt[1, 2][:], HALF + 2 * P, P)
+        quant_y(yt[1, 3][:], HALF + 3 * P, P)
+        store_words(HALF + 2 * P, 2 * P)
         store_scales()

from contextlib import ExitStack

import concourse.mybir as mybir
from concourse.masks import make_identity

T, D, F, E = 1024, 1536, 2048, 512
FLOPS = 2 * T * D * F + 2 * T * F * E

F32 = mybir.dt.float32
BF16 = mybir.dt.bfloat16
I32 = mybir.dt.int32
U32 = mybir.dt.uint32
U8 = mybir.dt.uint8
FP8X4 = mybir.dt.float8_e4m3fn_x4
FP4X4 = mybir.dt.float4_e2m1fn_x4
GELU = mybir.ActivationFunctionType.Gelu_apprx_tanh
COPY = mybir.ActivationFunctionType.Copy
ADD = mybir.AluOpType.add
MULT = mybir.AluOpType.mult

P = 128
PACK = 4
KP = P * PACK
HALF = 512
TILES = HALF // P
G1 = D // KP
G2 = F // KP


def tile_masked_token_embedding_head_h1_kernel(
    tc, x, w1_words, w1_scales, a, w2_words, w2_scales, b, c, r, out_0, out_1, out_2
):
    nc = tc.nc
    with ExitStack() as ctx:
        keep = ctx.enter_context(tc.tile_pool(name="keep", bufs=1))
        work = ctx.enter_context(tc.tile_pool(name="work", bufs=2))
        psum = ctx.enter_context(tc.psum_pool(name="psum", bufs=4))
        ctx.enter_context(tc.manual_schedule())

        def kept(name, shape, dtype):
            return keep.tile(shape, dtype, name=name, align_bytes=64)

        ident = kept("ident", [P, P], F32)
        make_identity(nc, ident[:])

        x_raw = {}
        xg = {}
        x_sorted = {}
        xq = {}
        xs = {}
        w1_raw = {}
        w1p = {}
        s1p = {}
        gel = {}
        hb = {}
        hc = {}
        hq = {}
        hs = {}
        zb = {}
        tb = {}
        ys = {}
        yb = {}
        ytb = {}

        s1_first = kept("s1_first", [P, G1, 2 * KP], U8)
        s1_rest = kept("s1_rest", [P, G1, F - 2 * KP], U8)
        s2 = kept("s2", [P, G2, E], U8)
        w2 = kept("w2", [P, G2, 2 * E], U8)
        a_sb = kept("a_sb", [P, G2, PACK], BF16)
        a32 = None
        b_sb = kept("b_sb", [P, E], BF16)
        c_sb = kept("c_sb", [P, E], BF16)
        r_sb = kept("r_sb", [P, T // P, 2], BF16)
        yq = kept("yq", [P, T], U32)
        yscale = kept("yscale", [P, T], U8)
        yt = {0: kept("yt0", [P, HALF * PACK], BF16)}
        yt[1, 0] = kept("yt1_0", [P, 2 * P * PACK], BF16)
        yt[1, 2] = kept("yt1_2", [P, P * PACK], BF16)
        yt[1, 3] = kept("yt1_3", [P, P * PACK], BF16)

        for plane in (s1_first, s1_rest, s2):
            nc.vector.memset(plane[:].rearrange("p g n -> p (g n)").bitcast(I32), 0)

        def load_x(h, g):
            x_raw[h, g] = kept("x_%d_%d" % (h, g), [P, TILES, KP], BF16)
            rows = x[h * HALF : (h + 1) * HALF, g * KP : (g + 1) * KP]
            nc.sync.dma_start(out=x_raw[h, g][:], in_=rows.rearrange("(i p) k -> p i k", p=P))

        def load_w1(G, g0, g1):
            raw = kept("w1_%d_%d" % (G, g0), [P, g1 - g0, 2 * KP], U8)
            src = w1_words[g0:g1, :, 2 * KP * G : 2 * KP * (G + 1)]
            nc.sync.dma_start(out=raw[:].bitcast(I32), in_=src.rearrange("g p n -> p g n").bitcast(I32))
            for g in range(g0, g1):
                w1_raw[G, g] = raw[:, g - g0, :]

        def load_scales(plane, rows):
            for q in range(4):
                nc.sync.dma_start(
                    out=plane[32 * q : 32 * q + 4, :, :].bitcast(I32),
                    in_=rows[:, 4 * q : 4 * q + 4, :].rearrange("g r n -> r g n").bitcast(I32),
                )

        def sort_scales(G, g):
            if G < 2:
                src = s1_first[:, g, G * KP : (G + 1) * KP]
            else:
                src = s1_rest[:, g, (G - 2) * KP : (G - 1) * KP]
            s1p[G, g] = kept("s1p_%d_%d" % (G, g), [P, PACK, P], U8)
            nc.vector.tensor_copy(out=s1p[G, g][:], in_=src.rearrange("p (m t) -> p t m", t=PACK))

        def sort_words(G, g):
            w1p[G, g] = kept("w1p_%d_%d" % (G, g), [P, PACK, 2 * P], U8)
            nc.vector.tensor_copy(
                out=w1p[G, g][:].rearrange("p t (m e) -> p t m e", e=2),
                in_=w1_raw[G, g].rearrange("p (m t e) -> p t m e", t=PACK, e=2),
            )

        def sort_group(G):
            for g in range(G1):
                sort_words(G, g)
                sort_scales(G, g)

        def sort_x(h, g, move=nc.scalar.copy):
            x_sorted[h, g] = work.tile([P, TILES, 2, P], F32, name="x_sorted", bufs=3)
            move(
                out=x_sorted[h, g][:],
                in_=x_raw[h, g][:].bitcast(F32).rearrange("n i (m u) -> n i u m", u=2),
            )

        def turn_x(h, g, second=nc.scalar.copy):
            xg[h, g] = work.tile([P, HALF * PACK], BF16, name="xg", bufs=3, align_bytes=64)
            dst = xg[h, g][:].bitcast(F32)
            for pair in range(TILES // 2):
                bank = psum.tile([P, 2, 2, P], F32, name="aux")
                for ii in range(2):
                    words = x_raw[h, g][:, 2 * pair + ii, :].bitcast(F32)
                    for u in range(2):
                        if (h, g) in x_sorted:
                            src = x_sorted[h, g][:, 2 * pair + ii, u, :]
                        else:
                            src = words[:, u : 2 * P : 2]
                        nc.tensor.transpose(bank[:, ii, u, :], src, ident[:])
                move = nc.scalar.copy if pair == 0 else second
                move(
                    out=dst[:, pair * KP : (pair + 1) * KP].rearrange("p (i n u) -> p i n u", i=2, u=2),
                    in_=bank[:].rearrange("p i u n -> p i n u"),
                )

        def quant_x(h, g):
            xq[h, g] = kept("xq_%d_%d" % (h, g), [P, HALF], U32)
            xs[h, g] = kept("xs_%d_%d" % (h, g), [P, HALF], U8)
            nc.vector.quantize_mx(out=xq[h, g][:].bitcast(FP8X4), scales=xs[h, g][:], in_=xg[h, g][:])

        def pass1(bank, h, G, g, t, cols):
            nc.tensor.matmul_mx(
                out=bank,
                lhsT=w1p[G, g][:, t, :].bitcast(FP4X4),
                lhsT_scale=s1p[G, g][:, t, :],
                rhs=xq[h, g][:, cols].bitcast(FP8X4),
                rhs_scale=xs[h, g][:, cols],
                start=(g == 0),
                stop=(g == G1 - 1),
            )

        def stage1(h, G, slots=range(PACK)):
            if slots[0] == 0:
                gel[h, G] = work.tile([P, PACK, HALF], F32, name="gel", bufs=4)
            for t in slots:
                bank = psum.tile([P, HALF], F32, name="s1")
                for g in range(G1):
                    pass1(bank[:], h, G, g, t, slice(0, HALF))
                nc.scalar.activation(out=gel[h, G][:, t, :], in_=bank[:], func=GELU)

        def scale_h(h, G):
            hb[h, G] = work.tile([P, HALF * PACK], BF16, name="hb", bufs=3, align_bytes=64)
            nc.vector.tensor_tensor(
                out=hb[h, G][:].rearrange("p (n i t) -> p n t i", i=2, t=PACK),
                in0=gel[h, G][:].rearrange("p t (n i) -> p n t i", i=2),
                in1=a_sb[:, G, :].unsqueeze(1).unsqueeze(3).broadcast_to([P, HALF // 2, PACK, 2]),
                op=MULT,
            )

        def scale_rows(h, G):
            hc[h, G] = work.tile([P, PACK, HALF], BF16, name="hc", bufs=2)
            for t in range(PACK):
                nc.scalar.activation(out=hc[h, G][:, t, :], in_=gel[h, G][:, t, :], func=COPY, scale=a32[:, G, t : t + 1])

        def weave_h(h, G):
            hb[h, G] = work.tile([P, HALF * PACK], BF16, name="hb", bufs=3, align_bytes=64)
            nc.vector.tensor_copy(
                out=hb[h, G][:].rearrange("p (n i t) -> p n t i", i=4, t=PACK),
                in_=hc[h, G][:].rearrange("p t (n i) -> p n t i", i=4),
            )

        def quant_h(h, G):
            hq[h, G] = kept("hq_%d_%d" % (h, G), [P, HALF], U32)
            hs[h, G] = kept("hs_%d_%d" % (h, G), [P, HALF], U8)
            nc.vector.quantize_mx(out=hq[h, G][:].bitcast(FP8X4), scales=hs[h, G][:], in_=hb[h, G][:])

        last = G2 - 1

        def stage1_tile(i):
            bank = psum.tile([P, PACK, P], F32, name="s1")
            for t in range(PACK):
                for g in range(G1):
                    pass1(bank[:, t, :], 1, last, g, t, slice(i * P, (i + 1) * P))
            gel[1, last, i] = work.tile([P, P, PACK], F32, name="gel_tile", bufs=4)
            nc.scalar.activation(out=gel[1, last, i][:], in_=bank[:].rearrange("p t n -> p n t"), func=GELU)

        def stage1_rows(i):
            bank = psum.tile([P, PACK, P], F32, name="s1")
            for t in range(PACK):
                for g in range(G1):
                    pass1(bank[:, t, :], 1, last, g, t, slice(i * P, (i + 1) * P))
            rows = work.tile([P, PACK, P], F32, name="gel_tile", bufs=4)
            nc.scalar.activation(out=rows[:], in_=bank[:], func=GELU)
            hc[1, last, i] = work.tile([P, PACK, P], BF16, name="hc_tile", bufs=4)
            for t in range(PACK):
                nc.scalar.activation(
                    out=hc[1, last, i][:, t, :], in_=rows[:, t, :], func=COPY, scale=a32[:, last, t : t + 1]
                )

        def weave_tile(i):
            hb[1, last, i] = work.tile([P, P * PACK], BF16, name="hb_tile", bufs=4, align_bytes=64)
            nc.vector.tensor_copy(
                out=hb[1, last, i][:].rearrange("p (n i t) -> p n t i", i=4, t=PACK),
                in_=hc[1, last, i][:].rearrange("p t (n i) -> p n t i", i=4),
            )

        def scale_tile(i):
            hb[1, last, i] = work.tile([P, P * PACK], BF16, name="hb_tile", bufs=4, align_bytes=64)
            nc.vector.tensor_tensor(
                out=hb[1, last, i][:].rearrange("p (n t) -> p n t", t=PACK),
                in0=gel[1, last, i][:],
                in1=a_sb[:, last, :].unsqueeze(1).broadcast_to([P, P, PACK]),
                op=MULT,
            )

        def quant_tile(i):
            hq[1, last, i] = kept("hq_tile_%d" % i, [P, P], U32)
            hs[1, last, i] = kept("hs_tile_%d" % i, [P, P], U8)
            nc.vector.quantize_mx(
                out=hq[1, last, i][:].bitcast(FP8X4), scales=hs[1, last, i][:], in_=hb[1, last, i][:]
            )

        def stage2(h, i, groups):
            for G in groups:
                if G == 0:
                    zb[h, i] = psum.tile([P, E], F32, name="aux")
                if (h, G, i) in hq:
                    codes, scales = hq[h, G, i][:], hs[h, G, i][:]
                else:
                    codes, scales = hq[h, G][:, i * P : (i + 1) * P], hs[h, G][:, i * P : (i + 1) * P]
                nc.tensor.matmul_mx(
                    out=zb[h, i][:],
                    lhsT=codes.bitcast(FP8X4),
                    lhsT_scale=scales,
                    rhs=w2[:, G, :].bitcast(FP4X4),
                    rhs_scale=s2[:, G, :],
                    start=(G == 0),
                    stop=(G == last),
                )

        def add_bias(h, i):
            tb[h, i] = work.tile([P, E], F32, name="tb", bufs=3)
            nc.vector.tensor_tensor(out=tb[h, i][:], in0=zb[h, i][:], in1=b_sb[:], op=ADD)

        def finish_y(h, i):
            j = h * TILES + i
            ys[h, i] = kept("y_%d" % j, [P, E], F32)
            nc.vector.scalar_tensor_tensor(
                out=ys[h, i][:], in0=tb[h, i][:], scalar=r_sb[:, j, 0:1], in1=c_sb[:], op0=MULT, op1=MULT
            )
            nc.sync.dma_start(out=out_0[j * P : (j + 1) * P, :], in_=ys[h, i][:])

        def round_y(h, i, move=nc.scalar.copy):
            yb[h, i] = work.tile([P, E], BF16, name="yb", bufs=4)
            move(
                out=yb[h, i][:].rearrange("n (u m e) -> n u m e", u=2, e=2),
                in_=ys[h, i][:].rearrange("n (m u e) -> n u m e", u=2, e=2),
            )

        def turn_y(h, tiles, dst):
            bank = psum.tile([P, 2, 2, P], F32, name="s1")
            for ii, i in enumerate(tiles):
                words = yb[h, i][:].bitcast(F32)
                for u in range(2):
                    nc.tensor.transpose(bank[:, ii, u, :], words[:, u * P : (u + 1) * P], ident[:])
            n = len(tiles)
            nc.scalar.copy(
                out=dst.bitcast(F32).rearrange("p (i n u) -> p i n u", i=n, u=2),
                in_=bank[:, 0:n, :, :].rearrange("p i u n -> p i n u"),
            )

        def quant_y(src, col0, cols):
            nc.vector.quantize_mx(
                out=yq[:, col0 : col0 + cols].bitcast(FP8X4), scales=yscale[:, col0 : col0 + cols], in_=src
            )

        def store_words(col0, cols):
            words = out_1[0].rearrange("p m t -> p (m t)").bitcast(I32)
            nc.sync.dma_start(out=words[:, col0 : col0 + cols], in_=yq[:, col0 : col0 + cols].bitcast(I32))

        def store_scales():
            for q in range(4):
                eng = nc.sync if q % 2 == 0 else nc.scalar
                eng.dma_start(
                    out=out_2[0, 4 * q : 4 * q + 4, :].bitcast(I32),
                    in_=yscale[32 * q : 32 * q + 4, :].bitcast(I32),
                )

        load_x(0, 0)
        load_scales(s1_first, w1_scales[:, :, 0 : 2 * KP])
        load_w1(0, 0, G1)
        load_x(0, 1)
        load_x(0, 2)
        load_w1(1, 0, G1)
        load_scales(s1_rest, w1_scales[:, :, 2 * KP : F])
        nc.sync.dma_start(out=a_sb[:], in_=a.rearrange("(g p t) -> p g t", p=P, t=PACK))
        load_x(1, 0)
        load_w1(2, 0, G1)
        load_x(1, 1)
        load_w1(3, 0, G1)
        load_x(1, 2)
        nc.sync.dma_start(out=w2[:].bitcast(I32), in_=w2_words.rearrange("g p n -> p g n").bitcast(I32))
        load_scales(s2, w2_scales)
        nc.sync.dma_start(out=b_sb[:], in_=b.partition_broadcast(P))
        nc.sync.dma_start(out=c_sb[:], in_=c.partition_broadcast(P))
        with nc.allow_non_contiguous_dma(reason="one value of r for each token partition"):
            nc.sync.dma_start(out=r_sb[:, :, 0:1], in_=r.rearrange("(j p o) -> p j o", p=P, o=1))

        for g in range(G1):
            sort_scales(0, g)
        turn_x(0, 0)
        turn_x(0, 1)
        turn_x(0, 2)
        sort_words(0, 0)
        sort_words(0, 1)
        sort_words(0, 2)
        quant_x(0, 0)
        for g in range(G1):
            sort_scales(1, g)
        banks = []
        for t in range(PACK):
            bank = psum.tile([P, HALF], F32, name="s1")
            banks.append(bank)
            pass1(bank[:], 0, 0, 0, t, slice(0, HALF))
        quant_x(0, 1)
        sort_words(1, 0)
        quant_x(0, 2)
        gel[0, 0] = work.tile([P, PACK, HALF], F32, name="gel", bufs=4)
        for t in range(PACK):
            pass1(banks[t][:], 0, 0, 1, t, slice(0, HALF))
            pass1(banks[t][:], 0, 0, 2, t, slice(0, HALF))
            nc.scalar.activation(out=gel[0, 0][:, t, :], in_=banks[t][:], func=GELU)

        sort_words(1, 1)
        sort_words(1, 2)
        sort_x(1, 0)
        stage1(0, 1)
        turn_x(1, 0)
        sort_group(2)
        scale_h(0, 0)
        stage1(0, 2, range(0, 2))
        sort_x(1, 2)
        stage1(0, 2, range(2, 4))
        turn_x(1, 1)
        sort_group(3)
        quant_h(0, 0)
        turn_x(1, 2)
        stage1(0, 3)
        scale_h(0, 1)
        quant_x(1, 0)
        quant_h(0, 1)
        quant_x(1, 1)
        quant_x(1, 2)
        scale_h(0, 2)
        stage1(1, 0)
        scale_h(0, 3)
        quant_h(0, 2)
        quant_h(0, 3)
        stage1(1, 1, range(0, 2))
        scale_h(1, 0)
        stage2(0, 0, range(G2))
        stage2(0, 1, range(G2))
        stage1(1, 1, range(2, 4))
        stage2(0, 2, range(G2))
        stage1(1, 2)
        add_bias(0, 0)
        quant_h(1, 0)
        add_bias(0, 1)
        finish_y(0, 0)
        finish_y(0, 1)
        scale_h(1, 1)
        add_bias(0, 2)
        quant_h(1, 1)
        finish_y(0, 2)
        stage2(0, 3, range(G2))
        scale_h(1, 2)
        add_bias(0, 3)
        quant_h(1, 2)
        finish_y(0, 3)
        round_y(0, 0)
        stage1_tile(0)
        round_y(0, 1)
        stage1_tile(1)
        round_y(0, 2)
        stage1_tile(2)
        stage1_tile(3)
        round_y(0, 3)
        stage2(1, 0, range(last))
        stage2(1, 1, range(last))
        scale_tile(0)
        scale_tile(1)
        quant_tile(0)
        scale_tile(2)
        quant_tile(1)
        stage2(1, 0, [last])
        stage2(1, 1, [last])
        turn_y(0, [0, 1], yt[0][:, 0 : 2 * KP])
        turn_y(0, [2, 3], yt[0][:, 2 * KP : 4 * KP])
        scale_tile(3)
        quant_tile(2)
        add_bias(1, 0)
        quant_tile(3)
        stage2(1, 2, range(G2))
        stage2(1, 3, range(G2))
        add_bias(1, 1)
        finish_y(1, 0)
        round_y(1, 0)
        finish_y(1, 1)
        round_y(1, 1)
        add_bias(1, 2)
        add_bias(1, 3)
        turn_y(1, [0, 1], yt[1, 0][:])
        finish_y(1, 2)
        round_y(1, 2)
        finish_y(1, 3)
        turn_y(1, [2], yt[1, 2][:])
        round_y(1, 3, nc.vector.tensor_copy)
        turn_y(1, [3], yt[1, 3][:])
        quant_y(yt[0][:], 0, HALF)
        store_words(0, HALF)
        quant_y(yt[1, 0][:], HALF, 2 * P)
        store_words(HALF, 2 * P)
        quant_y(yt[1, 2][:], HALF + 2 * P, P)
        quant_y(yt[1, 3][:], HALF + 3 * P, P)
        store_words(HALF + 2 * P, 2 * P)
        store_scales()
